import numpy as np
import ml_dtypes


def mxq(x, axis, fmt="e4m3"):
    dtype, down = {"e4m3": (ml_dtypes.float8_e4m3fn, 7), "e5m2": (ml_dtypes.float8_e5m2, 14)}[fmt]
    v = np.moveaxis(np.asarray(x, np.float32).astype(ml_dtypes.bfloat16).astype(np.float64), axis, -1)
    blocks = v.reshape(v.shape[:-1] + (-1, 32))
    amax = np.abs(blocks).max(-1, keepdims=True)
    byte = np.maximum(np.where(amax > 0, np.frexp(amax)[1] - 1 + 127, 0) - down, 1)
    scale = np.exp2(byte - 127.0)
    codes = (blocks / scale).astype(np.float32).astype(dtype).astype(np.float64)
    return np.moveaxis((codes * scale).reshape(v.shape), -1, axis)


WIDE = False


def mx_kscale(k):
    if not WIDE:
        return np.ones(k)
    levels = np.array([10, -10, 5, -5, 0])
    if k % 512:
        return np.exp2(np.random.permutation(np.resize(levels, k // 32))).repeat(32)
    a = np.empty((k // 512, 16))
    for p in range(k // 512):
        a[p, :8] = np.random.permutation(np.resize(levels, 8))
        for g in range(8):
            far = levels[np.abs(levels - a[p, g]) >= 10]
            a[p, g + 8] = far[np.random.randint(len(far))]
    return np.exp2(a.ravel()).repeat(32)


def f64(x):
    return np.asarray(x).astype(np.float64)


def striped(idx):
    return np.tile(idx.reshape(-1, 16).T, (8, 1)).astype(np.uint16)


def unstriped(offs):
    return offs[:16].T.reshape(-1).astype(np.int64)


def pack_weight(w):
    k, n = w.shape
    w = f64(np.asarray(w, np.float32).astype(ml_dtypes.bfloat16)).reshape(k // 32, 32, n)
    amax = np.abs(w).max(1)
    byte = np.clip(np.where(amax > 0, np.frexp(amax)[1] - 1 + 127 - 7, 1), 1, 254)
    scaled = (w * np.exp2(127.0 - byte)[:, None, :]).reshape(k, n).astype(np.float32)
    words = np.ascontiguousarray(scaled.reshape(k // 512, 128, 4, n).transpose(0, 1, 3, 2)).astype(ml_dtypes.float8_e4m3fn).view(np.uint8)
    return words, np.ascontiguousarray(byte.astype(np.uint8).reshape(k // 512, 16, n))


def unpack_weight(words, scales):
    g, p, n, _ = words.shape
    vals = np.ascontiguousarray(words).view(ml_dtypes.float8_e4m3fn).astype(np.float64) * np.repeat(np.exp2(scales.astype(np.float64) - 127.0), 8, axis=1)[..., None]
    return vals.transpose(0, 1, 3, 2).reshape(g * 512, n)


K, T, S, D, N, R = 1024, 1024, 512, 4, 128, 256


def setup_inputs():
    n = np.random.standard_normal
    s = mx_kscale(K)[:, None]
    packed_xT = pack_weight(n((K, T)) * s)
    return {
        "x_words": packed_xT[0],
        "x_scales": packed_xT[1],
        "w1": (n((K, N)) / np.sqrt(K) / s).astype(np.float32),
        "flow": (n((N, R))).astype(np.float32),
        "offs": striped(np.random.permutation(T)[:S]),
        "nbr": striped(np.random.permutation(np.concatenate([np.arange(R), np.random.randint(0, R, S - R)]))),
    }


def reference(x_words, x_scales, w1, flow, offs, nbr):
    xq = unpack_weight(x_words, x_scales)[:, unstriped(offs)]
    y = mxq(f64(w1), 0, "e4m3").T @ xq
    top = y.reshape(len(y), -1, D).max(axis=2)
    ex = np.exp(y - np.repeat(top, D, axis=1))
    total = ex.reshape(len(ex), -1, D).sum(axis=2)
    mask = ex / np.repeat(total, D, axis=1)
    mf = mask * f64(flow)[:, unstriped(nbr)]
    up = mf.reshape(len(mf), -1, D).sum(axis=2)
    dv = mask * ((f64(flow)[:, unstriped(nbr)] - np.repeat(up, D, axis=1)) ** 2)
    return 8.0 * (up * (-1.0 * (0.3 * (dv.reshape(len(dv), -1, D).sum(axis=2))) + 1.0))

@@ -1,0 +1,146 @@
+from contextlib import ExitStack
+
+import concourse.mybir as mybir
+
+K, T, S, D, N, R = 1024, 1024, 512, 4, 128, 256
+FLOPS = 2 * K * N * S
+
+F32 = mybir.dt.float32
+BF16 = mybir.dt.bfloat16
+I32 = mybir.dt.int32
+U32 = mybir.dt.uint32
+U16 = mybir.dt.uint16
+U8 = mybir.dt.uint8
+FP8X4 = mybir.dt.float8_e4m3fn_x4
+ALU = mybir.AluOpType
+ACT = mybir.ActivationFunctionType
+AXIS_X = mybir.AxisListType.X
+
+P = 128
+PACK = 4
+PASSES = K // (P * PACK)
+HALVES = 2
+HS = S // HALVES
+HV = HS // D
+FLOW_WINDOW = 768
+
+
+def tile_picked_yraft_conf_p_kernel(tc, x_words, x_scales, w1, flow, offs, nbr, out):
+    nc = tc.nc
+    with ExitStack() as ctx:
+        pool = ctx.enter_context(tc.tile_pool(name="held", bufs=1))
+        psum = ctx.enter_context(tc.psum_pool(name="psum", bufs=1))
+
+        nbr_list = pool.tile([P, S // 16], U16, name="nbr_list")
+        offs_list = pool.tile([P, S // 16], U16, name="offs_list")
+        flow_window = pool.tile([P, FLOW_WINDOW], F32, name="flow_window")
+        scale_window = pool.tile([P, T], U8, name="scale_window", align_bytes=64)
+        word_windows = [pool.tile([P, T], I32, name="word_window%d" % o, align_bytes=64) for o in range(PASSES)]
+        w_raw = [pool.tile([P, PACK, N], F32, name="w_raw%d" % o) for o in range(PASSES)]
+        warm = pool.tile([P, 2], F32, name="warm")
+
+        nc.vector.memset(scale_window[:].bitcast(I32), 0)
+        nc.gpsimd.memset(flow_window[:, R:], 0.0)
+        nc.gpsimd.memset(warm[:, 0:1], 0.0)
+
+        nc.sync.dma_start(nbr_list[:], nbr)
+        nc.sync.dma_start(flow_window[:, :R], flow)
+        nc.sync.dma_start(offs_list[:], offs)
+        for q in range(4):
+            nc.scalar.dma_start(
+                scale_window[32 * q : 32 * q + 4 * PASSES, :].bitcast(I32),
+                x_scales[:, 4 * q : 4 * q + 4, :].bitcast(I32),
+            )
+        nc.scalar.activation(warm[:, 1:2], warm[:, 0:1], ACT.Exp)
+
+        def load_words(o):
+            nc.sync.dma_start(word_windows[o][:], x_words[o].rearrange("p n t -> p (n t)").bitcast(I32))
+
+        load_words(0)
+        for o in range(PASSES):
+            rows = w1[o * P * PACK : (o + 1) * P * PACK, :]
+            nc.sync.dma_start(w_raw[o][:], rows.rearrange("(p j) n -> p j n", j=PACK))
+        load_words(1)
+
+        f = pool.tile([P, S], F32, name="f")
+        nc.vector.tensor_copy(f[:], flow_window[:].indirect(nbr_list[:]))
+        x_planes = pool.tile([P, S], U8, name="x_planes", align_bytes=64)
+        nc.vector.tensor_copy(x_planes[:], scale_window[:].indirect(offs_list[:]))
+
+        w_grouped = pool.tile([P, PASSES, N, PACK], BF16, name="w_grouped", align_bytes=64)
+        for o in range(PASSES):
+            nc.scalar.copy(w_grouped[:, o], w_raw[o][:].rearrange("p j n -> p n j"))
+        w_codes = pool.tile([P, PASSES * N], U32, name="w_codes", align_bytes=64)
+        w_scales = pool.tile([P, PASSES * N], U8, name="w_scales", align_bytes=64)
+
+        x_codes = [
+            [pool.tile([P, HS], U32, name="x_codes%d_%d" % (o, h), align_bytes=64) for h in range(HALVES)]
+            for o in range(PASSES)
+        ]
+
+        def gather_words(o, h):
+            piece = offs_list[:, h * HS // 16 : (h + 1) * HS // 16]
+            nc.vector.tensor_copy(x_codes[o][h][:], word_windows[o][:].bitcast(U32).indirect(piece))
+
+        gather_words(0, 0)
+        gather_words(0, 1)
+        nc.vector.quantize_mx(
+            out=w_codes[:].bitcast(FP8X4),
+            scales=w_scales[:],
+            in_=w_grouped[:].rearrange("p o n j -> p (o n j)"),
+        )
+        logits = [psum.tile([P, HS], F32, name="logits%d" % h) for h in range(HALVES)]
+        for h in range(HALVES):
+            gather_words(1, h)
+            for o in range(PASSES):
+                nc.tensor.matmul_mx(
+                    out=logits[h][:],
+                    lhsT=w_codes[:, o * N : (o + 1) * N].bitcast(FP8X4),
+                    lhsT_scale=w_scales[:, o * N : (o + 1) * N],
+                    rhs=x_codes[o][h][:].bitcast(FP8X4),
+                    rhs_scale=x_planes[4 * o : P, h * HS : (h + 1) * HS],
+                    start=(o == 0),
+                    stop=(o == PASSES - 1),
+                )
+
+        def tiles(name, shape):
+            return [pool.tile(shape, F32, name="%s%d" % (name, h)) for h in range(HALVES)]
+
+        def groups(ap):
+            return ap.rearrange("p (v d) -> p v d", d=D)
+
+        def spread(ap):
+            return ap.unsqueeze(2).to_broadcast([P, HV, D])
+
+        top, z = tiles("top", [P, HV]), tiles("z", [P, HS])
+        terms, sums = tiles("terms", [P, 2 * HS]), tiles("sums", [P, 2 * HV])
+        inv, up, spreadsq = tiles("inv", [P, HV]), tiles("up", [P, HV]), tiles("spreadsq", [P, HV])
+        dev, dev2, wdev2 = tiles("dev", [P, HS]), tiles("dev2", [P, HS]), tiles("wdev2", [P, HS])
+        damp, res = tiles("damp", [P, HV]), tiles("res", [P, HV])
+        both = range(HALVES)
+
+        for h in both:
+            nc.vector.tensor_reduce(top[h][:], groups(logits[h][:]), AXIS_X, ALU.max)
+        for h in both:
+            nc.vector.tensor_tensor(groups(z[h][:]), groups(logits[h][:]), spread(top[h][:]), ALU.subtract)
+            nc.scalar.activation(terms[h][:, :HS], z[h][:], ACT.Exp)
+        for h in both:
+            nc.vector.tensor_tensor(terms[h][:, HS:], terms[h][:, :HS], f[:, h * HS : (h + 1) * HS], ALU.mult)
+        for h in both:
+            nc.vector.tensor_reduce(sums[h][:], groups(terms[h][:]), AXIS_X, ALU.add)
+        for h in both:
+            nc.vector.reciprocal(inv[h][:], sums[h][:, :HV])
+        for h in both:
+            nc.vector.tensor_tensor(up[h][:], sums[h][:, HV:], inv[h][:], ALU.mult)
+        for h in both:
+            nc.vector.tensor_tensor(groups(dev[h][:]), groups(f[:, h * HS : (h + 1) * HS]), spread(up[h][:]), ALU.subtract)
+            nc.scalar.activation(dev2[h][:], dev[h][:], ACT.Square)
+        for h in both:
+            nc.vector.tensor_tensor(wdev2[h][:], dev2[h][:], terms[h][:, :HS], ALU.mult)
+        for h in both:
+            nc.vector.tensor_reduce(spreadsq[h][:], groups(wdev2[h][:]), AXIS_X, ALU.add)
+        for h in both:
+            nc.vector.scalar_tensor_tensor(damp[h][:], spreadsq[h][:], -0.3 * 8.0, inv[h][:], ALU.mult, ALU.mult)
+        for h in both:
+            nc.vector.scalar_tensor_tensor(res[h][:], damp[h][:], 8.0, up[h][:], ALU.add, ALU.mult)
+            nc.sync.dma_start(out[:, h * HV : (h + 1) * HV], res[h][:])

@@ -67,11 +67,11 @@ def tile_picked_yraft_conf_p_kernel(tc, x_words, x_scales, w1, flow, offs, nbr, 
         x_planes = pool.tile([P, S], U8, name="x_planes", align_bytes=64)
         nc.vector.tensor_copy(x_planes[:], scale_window[:].indirect(offs_list[:]))
 
-        w_grouped = pool.tile([P, PASSES, N, PACK], BF16, name="w_grouped", align_bytes=64)
+        w_grouped = [pool.tile([P, N, PACK], BF16, name="w_grouped%d" % o, align_bytes=64) for o in range(PASSES)]
         for o in range(PASSES):
-            nc.scalar.copy(w_grouped[:, o], w_raw[o][:].rearrange("p j n -> p n j"))
-        w_codes = pool.tile([P, PASSES * N], U32, name="w_codes", align_bytes=64)
-        w_scales = pool.tile([P, PASSES * N], U8, name="w_scales", align_bytes=64)
+            nc.scalar.copy(w_grouped[o][:], w_raw[o][:].rearrange("p j n -> p n j"))
+        w_codes = [pool.tile([P, N], U32, name="w_codes%d" % o, align_bytes=64) for o in range(PASSES)]
+        w_scales = [pool.tile([P, N], U8, name="w_scales%d" % o, align_bytes=64) for o in range(PASSES)]
 
         x_codes = [
             [pool.tile([P, HS], U32, name="x_codes%d_%d" % (o, h), align_bytes=64) for h in range(HALVES)]
@@ -84,19 +84,20 @@ def tile_picked_yraft_conf_p_kernel(tc, x_words, x_scales, w1, flow, offs, nbr, 
 
         gather_words(0, 0)
         gather_words(0, 1)
-        nc.vector.quantize_mx(
-            out=w_codes[:].bitcast(FP8X4),
-            scales=w_scales[:],
-            in_=w_grouped[:].rearrange("p o n j -> p (o n j)"),
-        )
+        for o in range(PASSES):
+            nc.vector.quantize_mx(
+                out=w_codes[o][:].bitcast(FP8X4),
+                scales=w_scales[o][:],
+                in_=w_grouped[o][:].rearrange("p n j -> p (n j)"),
+            )
         logits = [psum.tile([P, HS], F32, name="logits%d" % h) for h in range(HALVES)]
         for h in range(HALVES):
             gather_words(1, h)
             for o in range(PASSES):
                 nc.tensor.matmul_mx(
                     out=logits[h][:],
-                    lhsT=w_codes[:, o * N : (o + 1) * N].bitcast(FP8X4),
-                    lhsT_scale=w_scales[:, o * N : (o + 1) * N],
+                    lhsT=w_codes[o][:].bitcast(FP8X4),
+                    lhsT_scale=w_scales[o][:],
                     rhs=x_codes[o][h][:].bitcast(FP8X4),
                     rhs_scale=x_planes[4 * o : P, h * HS : (h + 1) * HS],
                     start=(o == 0),
@@ -114,33 +115,66 @@ def tile_picked_yraft_conf_p_kernel(tc, x_words, x_scales, w1, flow, offs, nbr, 
 
         top, z = tiles("top", [P, HV]), tiles("z", [P, HS])
         terms, sums = tiles("terms", [P, 2 * HS]), tiles("sums", [P, 2 * HV])
-        inv, up, spreadsq = tiles("inv", [P, HV]), tiles("up", [P, HV]), tiles("spreadsq", [P, HV])
+        inv, up, gain = tiles("inv", [P, HV]), tiles("up", [P, HV]), tiles("gain", [P, HV])
         dev, dev2, wdev2 = tiles("dev", [P, HS]), tiles("dev2", [P, HS]), tiles("wdev2", [P, HS])
-        damp, res = tiles("damp", [P, HV]), tiles("res", [P, HV])
-        both = range(HALVES)
+        share, res = tiles("share", [P, HS]), tiles("res", [P, HV])
 
-        for h in both:
+        def shift(h):
             nc.vector.tensor_reduce(top[h][:], groups(logits[h][:]), AXIS_X, ALU.max)
-        for h in both:
             nc.vector.tensor_tensor(groups(z[h][:]), groups(logits[h][:]), spread(top[h][:]), ALU.subtract)
             nc.scalar.activation(terms[h][:, :HS], z[h][:], ACT.Exp)
-        for h in both:
-            nc.vector.tensor_tensor(terms[h][:, HS:], terms[h][:, :HS], f[:, h * HS : (h + 1) * HS], ALU.mult)
-        for h in both:
-            nc.vector.tensor_reduce(sums[h][:], groups(terms[h][:]), AXIS_X, ALU.add)
-        for h in both:
+
+        def total(h):
+            nc.vector.tensor_reduce(sums[h][:, :HV], groups(terms[h][:, :HS]), AXIS_X, ALU.add)
+
+        def weigh(h):
+            nc.gpsimd.tensor_tensor(terms[h][:, HS:], terms[h][:, :HS], f[:, h * HS : (h + 1) * HS], ALU.mult)
+
+        def invert(h):
             nc.vector.reciprocal(inv[h][:], sums[h][:, :HV])
-        for h in both:
+
+        def weighted_sum(h):
+            nc.vector.tensor_reduce(sums[h][:, HV:], groups(terms[h][:, HS:]), AXIS_X, ALU.add)
+
+        def mean(h):
             nc.vector.tensor_tensor(up[h][:], sums[h][:, HV:], inv[h][:], ALU.mult)
-        for h in both:
+
+        def deviate(h):
             nc.vector.tensor_tensor(groups(dev[h][:]), groups(f[:, h * HS : (h + 1) * HS]), spread(up[h][:]), ALU.subtract)
             nc.scalar.activation(dev2[h][:], dev[h][:], ACT.Square)
-        for h in both:
-            nc.vector.tensor_tensor(wdev2[h][:], dev2[h][:], terms[h][:, :HS], ALU.mult)
-        for h in both:
-            nc.vector.tensor_reduce(spreadsq[h][:], groups(wdev2[h][:]), AXIS_X, ALU.add)
-        for h in both:
-            nc.vector.scalar_tensor_tensor(damp[h][:], spreadsq[h][:], -0.3 * 8.0, inv[h][:], ALU.mult, ALU.mult)
-        for h in both:
-            nc.vector.scalar_tensor_tensor(res[h][:], damp[h][:], 8.0, up[h][:], ALU.add, ALU.mult)
+
+        def group_gain(h):
+            nc.vector.scalar_tensor_tensor(gain[h][:], up[h][:], -0.3 * 8.0, inv[h][:], ALU.mult, ALU.mult)
+
+        def entry_share(h):
+            nc.vector.tensor_tensor(groups(share[h][:]), groups(terms[h][:, :HS]), spread(gain[h][:]), ALU.mult)
+
+        def weigh_dev(h):
+            nc.vector.scalar_tensor_tensor(wdev2[h][:], dev2[h][:], -1.0 / 0.3, share[h][:], ALU.add, ALU.mult)
+
+        def finish(h):
+            nc.vector.tensor_reduce(res[h][:], groups(wdev2[h][:]), AXIS_X, ALU.add)
             nc.sync.dma_start(out[:, h * HV : (h + 1) * HV], res[h][:])
+
+        shift(0)
+        shift(1)
+        weigh(0)
+        weigh(1)
+        total(0)
+        invert(0)
+        total(1)
+        weighted_sum(0)
+        invert(1)
+        mean(0)
+        weighted_sum(1)
+        group_gain(0)
+        deviate(0)
+        mean(1)
+        entry_share(0)
+        group_gain(1)
+        deviate(1)
+        entry_share(1)
+        weigh_dev(0)
+        weigh_dev(1)
+        finish(0)
+        finish(1)

from contextlib import ExitStack

import concourse.mybir as mybir

K, T, S, D, N, R = 1024, 1024, 512, 4, 128, 256
FLOPS = 2 * K * N * S

F32 = mybir.dt.float32
BF16 = mybir.dt.bfloat16
I32 = mybir.dt.int32
U32 = mybir.dt.uint32
U16 = mybir.dt.uint16
U8 = mybir.dt.uint8
FP8X4 = mybir.dt.float8_e4m3fn_x4
ALU = mybir.AluOpType
ACT = mybir.ActivationFunctionType
AXIS_X = mybir.AxisListType.X

P = 128
PACK = 4
PASSES = K // (P * PACK)
HALVES = 2
HS = S // HALVES
HV = HS // D
FLOW_WINDOW = 768


def tile_picked_yraft_conf_p_kernel(tc, x_words, x_scales, w1, flow, offs, nbr, out):
    nc = tc.nc
    with ExitStack() as ctx:
        pool = ctx.enter_context(tc.tile_pool(name="held", bufs=1))
        psum = ctx.enter_context(tc.psum_pool(name="psum", bufs=1))

        nbr_list = pool.tile([P, S // 16], U16, name="nbr_list")
        offs_list = pool.tile([P, S // 16], U16, name="offs_list")
        flow_window = pool.tile([P, FLOW_WINDOW], F32, name="flow_window")
        scale_window = pool.tile([P, T], U8, name="scale_window", align_bytes=64)
        word_windows = [pool.tile([P, T], I32, name="word_window%d" % o, align_bytes=64) for o in range(PASSES)]
        w_raw = [pool.tile([P, PACK, N], F32, name="w_raw%d" % o) for o in range(PASSES)]
        warm = pool.tile([P, 2], F32, name="warm")

        nc.vector.memset(scale_window[:].bitcast(I32), 0)
        nc.gpsimd.memset(flow_window[:, R:], 0.0)
        nc.gpsimd.memset(warm[:, 0:1], 0.0)

        nc.sync.dma_start(nbr_list[:], nbr)
        nc.sync.dma_start(flow_window[:, :R], flow)
        nc.sync.dma_start(offs_list[:], offs)
        for q in range(4):
            nc.scalar.dma_start(
                scale_window[32 * q : 32 * q + 4 * PASSES, :].bitcast(I32),
                x_scales[:, 4 * q : 4 * q + 4, :].bitcast(I32),
            )
        nc.scalar.activation(warm[:, 1:2], warm[:, 0:1], ACT.Exp)

        def load_words(o):
            nc.sync.dma_start(word_windows[o][:], x_words[o].rearrange("p n t -> p (n t)").bitcast(I32))

        load_words(0)
        for o in range(PASSES):
            rows = w1[o * P * PACK : (o + 1) * P * PACK, :]
            nc.sync.dma_start(w_raw[o][:], rows.rearrange("(p j) n -> p j n", j=PACK))
        load_words(1)

        f = pool.tile([P, S], F32, name="f")
        nc.vector.tensor_copy(f[:], flow_window[:].indirect(nbr_list[:]))
        x_planes = pool.tile([P, S], U8, name="x_planes", align_bytes=64)
        nc.vector.tensor_copy(x_planes[:], scale_window[:].indirect(offs_list[:]))

        w_grouped = [pool.tile([P, N, PACK], BF16, name="w_grouped%d" % o, align_bytes=64) for o in range(PASSES)]
        for o in range(PASSES):
            nc.scalar.copy(w_grouped[o][:], w_raw[o][:].rearrange("p j n -> p n j"))
        w_codes = [pool.tile([P, N], U32, name="w_codes%d" % o, align_bytes=64) for o in range(PASSES)]
        w_scales = [pool.tile([P, N], U8, name="w_scales%d" % o, align_bytes=64) for o in range(PASSES)]

        x_codes = [
            [pool.tile([P, HS], U32, name="x_codes%d_%d" % (o, h), align_bytes=64) for h in range(HALVES)]
            for o in range(PASSES)
        ]

        def gather_words(o, h):
            piece = offs_list[:, h * HS // 16 : (h + 1) * HS // 16]
            nc.vector.tensor_copy(x_codes[o][h][:], word_windows[o][:].bitcast(U32).indirect(piece))

        gather_words(0, 0)
        gather_words(0, 1)
        for o in range(PASSES):
            nc.vector.quantize_mx(
                out=w_codes[o][:].bitcast(FP8X4),
                scales=w_scales[o][:],
                in_=w_grouped[o][:].rearrange("p n j -> p (n j)"),
            )
        logits = [psum.tile([P, HS], F32, name="logits%d" % h) for h in range(HALVES)]
        for h in range(HALVES):
            gather_words(1, h)
            for o in range(PASSES):
                nc.tensor.matmul_mx(
                    out=logits[h][:],
                    lhsT=w_codes[o][:].bitcast(FP8X4),
                    lhsT_scale=w_scales[o][:],
                    rhs=x_codes[o][h][:].bitcast(FP8X4),
                    rhs_scale=x_planes[4 * o : P, h * HS : (h + 1) * HS],
                    start=(o == 0),
                    stop=(o == PASSES - 1),
                )

        def tiles(name, shape):
            return [pool.tile(shape, F32, name="%s%d" % (name, h)) for h in range(HALVES)]

        def groups(ap):
            return ap.rearrange("p (v d) -> p v d", d=D)

        def spread(ap):
            return ap.unsqueeze(2).to_broadcast([P, HV, D])

        top, z = tiles("top", [P, HV]), tiles("z", [P, HS])
        terms, sums = tiles("terms", [P, 2 * HS]), tiles("sums", [P, 2 * HV])
        inv, up, gain = tiles("inv", [P, HV]), tiles("up", [P, HV]), tiles("gain", [P, HV])
        dev, dev2, wdev2 = tiles("dev", [P, HS]), tiles("dev2", [P, HS]), tiles("wdev2", [P, HS])
        share, res = tiles("share", [P, HS]), tiles("res", [P, HV])

        def shift(h):
            nc.vector.tensor_reduce(top[h][:], groups(logits[h][:]), AXIS_X, ALU.max)
            nc.vector.tensor_tensor(groups(z[h][:]), groups(logits[h][:]), spread(top[h][:]), ALU.subtract)
            nc.scalar.activation(terms[h][:, :HS], z[h][:], ACT.Exp)

        def total(h):
            nc.vector.tensor_reduce(sums[h][:, :HV], groups(terms[h][:, :HS]), AXIS_X, ALU.add)

        def weigh(h):
            nc.gpsimd.tensor_tensor(terms[h][:, HS:], terms[h][:, :HS], f[:, h * HS : (h + 1) * HS], ALU.mult)

        def invert(h):
            nc.vector.reciprocal(inv[h][:], sums[h][:, :HV])

        def weighted_sum(h):
            nc.vector.tensor_reduce(sums[h][:, HV:], groups(terms[h][:, HS:]), AXIS_X, ALU.add)

        def mean(h):
            nc.vector.tensor_tensor(up[h][:], sums[h][:, HV:], inv[h][:], ALU.mult)

        def deviate(h):
            nc.vector.tensor_tensor(groups(dev[h][:]), groups(f[:, h * HS : (h + 1) * HS]), spread(up[h][:]), ALU.subtract)
            nc.scalar.activation(dev2[h][:], dev[h][:], ACT.Square)

        def group_gain(h):
            nc.vector.scalar_tensor_tensor(gain[h][:], up[h][:], -0.3 * 8.0, inv[h][:], ALU.mult, ALU.mult)

        def entry_share(h):
            nc.vector.tensor_tensor(groups(share[h][:]), groups(terms[h][:, :HS]), spread(gain[h][:]), ALU.mult)

        def weigh_dev(h):
            nc.vector.scalar_tensor_tensor(wdev2[h][:], dev2[h][:], -1.0 / 0.3, share[h][:], ALU.add, ALU.mult)

        def finish(h):
            nc.vector.tensor_reduce(res[h][:], groups(wdev2[h][:]), AXIS_X, ALU.add)
            nc.sync.dma_start(out[:, h * HV : (h + 1) * HV], res[h][:])

        shift(0)
        shift(1)
        weigh(0)
        weigh(1)
        total(0)
        invert(0)
        total(1)
        weighted_sum(0)
        invert(1)
        mean(0)
        weighted_sum(1)
        group_gain(0)
        deviate(0)
        mean(1)
        entry_share(0)
        group_gain(1)
        deviate(1)
        entry_share(1)
        weigh_dev(0)
        weigh_dev(1)
        finish(0)
        finish(1)
